import numpy as np
import ml_dtypes


def mxq(x, axis, fmt="e4m3"):
    dtype, down = {"e4m3": (ml_dtypes.float8_e4m3fn, 7), "e5m2": (ml_dtypes.float8_e5m2, 14)}[fmt]
    v = np.moveaxis(np.asarray(x, np.float32).astype(ml_dtypes.bfloat16).astype(np.float64), axis, -1)
    blocks = v.reshape(v.shape[:-1] + (-1, 32))
    amax = np.abs(blocks).max(-1, keepdims=True)
    byte = np.maximum(np.where(amax > 0, np.frexp(amax)[1] - 1 + 127, 0) - down, 1)
    scale = np.exp2(byte - 127.0)
    codes = (blocks / scale).astype(np.float32).astype(dtype).astype(np.float64)
    return np.moveaxis((codes * scale).reshape(v.shape), -1, axis)


WIDE = False


def mx_kscale(k):
    if not WIDE:
        return np.ones(k)
    levels = np.array([10, -10, 5, -5, 0])
    if k % 512:
        return np.exp2(np.random.permutation(np.resize(levels, k // 32))).repeat(32)
    a = np.empty((k // 512, 16))
    for p in range(k // 512):
        a[p, :8] = np.random.permutation(np.resize(levels, 8))
        for g in range(8):
            far = levels[np.abs(levels - a[p, g]) >= 10]
            a[p, g + 8] = far[np.random.randint(len(far))]
    return np.exp2(a.ravel()).repeat(32)


def f64(x):
    return np.asarray(x).astype(np.float64)


def striped(idx):
    return np.tile(np.asarray(idx).reshape(-1, 16).T, (8, 1)).astype(np.uint16)


def unstriped(offs):
    return offs[:16].T.reshape(-1).astype(np.int64)


def striped8(idx):
    return np.asarray(idx).reshape(8, -1, 16).transpose(0, 2, 1).reshape(128, -1).astype(np.uint16)


def unstriped8(offs):
    return offs.reshape(8, 16, -1).transpose(0, 2, 1).reshape(8, -1).astype(np.int64)


def pick8(x, idx, run):
    r = np.arange(len(x))
    return x[r[:, None], idx[r % (8 * run) // run]]


E2M1 = np.array([0.0, 0.5, 1.0, 1.5, 2.0, 3.0, 4.0, 6.0, -0.0, -0.5, -1.0, -1.5, -2.0, -3.0, -4.0, -6.0])


def pack_weight(w, fmt):
    k, n = w.shape
    w = f64(np.asarray(w, np.float32).astype(ml_dtypes.bfloat16)).reshape(k // 32, 32, n)
    amax = np.abs(w).max(1)
    if fmt == "e4m3":
        byte = np.frexp(amax)[1] - 1 + 127 - 7
    else:
        mant, ex = np.frexp(amax / 6.0)
        byte = np.where(mant > 0.5, ex, ex - 1) + 127
    byte = np.clip(np.where(amax > 0, byte, 1), 1, 254)
    scaled = (w * np.exp2(127.0 - byte)[:, None, :]).reshape(k, n).astype(np.float32)
    by_word = np.ascontiguousarray(scaled.reshape(k // 512, 128, 4, n).transpose(0, 1, 3, 2))
    if fmt == "e4m3":
        words = by_word.astype(ml_dtypes.float8_e4m3fn).view(np.uint8)
    else:
        c = by_word.astype(ml_dtypes.float4_e2m1fn).view(np.uint8) & 0xF
        words = (c[..., 0::2] | (c[..., 1::2] << 4)).reshape(k // 512, 128, 2 * n)
    return np.ascontiguousarray(words), np.ascontiguousarray(byte.astype(np.uint8).reshape(k // 512, 16, n))


def unpack_weight(words, scales, fmt):
    g, _, n = scales.shape
    words = np.ascontiguousarray(words).reshape(g, 128, n, -1)
    if fmt == "e4m3":
        vals = words.view(ml_dtypes.float8_e4m3fn).astype(np.float64)
    else:
        nib = np.empty((g, 128, n, 4), np.uint8)
        nib[..., 0::2] = words & 0xF
        nib[..., 1::2] = words >> 4
        vals = E2M1[nib]
    vals = vals * np.repeat(np.exp2(scales.astype(np.float64) - 127.0), 8, axis=1)[..., None]
    return vals.transpose(0, 1, 3, 2).reshape(g * 512, n)


K, J, R, T, F, Z, M, O, C, N, S, V = 512, 256, 512, 512, 2048, 512, 1024, 128, 512, 256, 512, 1024


def setup_inputs():
    n = np.random.standard_normal
    idx = np.random.permutation(T)[:J]
    idx2 = np.stack([np.random.permutation(F)[:R] for _ in range(8)])
    idx3 = np.random.permutation(M)[:J]
    idx4 = np.stack([np.random.permutation(C)[:J] for _ in range(8)])
    idx5 = np.stack([np.random.permutation(C)[:J] for _ in range(8)])
    idx6 = np.stack([np.random.permutation(J)[:O] for _ in range(8)])
    idx7 = np.random.permutation(V)[:O]
    fk = mx_kscale(K)
    fz = mx_kscale(Z)
    fr = mx_kscale(R)
    fs = mx_kscale(S)
    xtp = pack_weight(n((K, T)) * fk[:, None], "e2m1")
    xop = pack_weight(n((Z, M)) / fz[:, None], "e4m3")
    w2p = pack_weight(n((Z, R)) * 1 / np.sqrt(Z) * fz[:, None], "e2m1")
    wbp = pack_weight(n((R, N)) * 1 / np.sqrt(R) / fr[:, None], "e2m1")
    xrp = pack_weight(n((S, V)) / fs[:, None], "e4m3")
    wsp = pack_weight(n((S, N)) * 1 / np.sqrt(S) * fs[:, None], "e4m3")
    return {
        "xt_words": xtp[0],
        "xt_scales": xtp[1],
        "ua": (np.random.randint(-7, 8, (K, F)).astype(np.float64)).astype(np.float32),
        "ha": ((np.random.randint(8, 25, (K, 1)) / 1024.0) / fk[:, None]).astype(np.float32),
        "xo_words": xop[0],
        "xo_scales": xop[1],
        "w2_words": w2p[0],
        "w2_scales": w2p[1],
        "sa": (np.random.uniform(0.5, 1.6, (R, 1))).astype(np.float32),
        "sb": (np.random.uniform(0.5, 1.6, (R, 1)) * fr[:, None]).astype(np.float32),
        "wb_words": wbp[0],
        "wb_scales": wbp[1],
        "xr_words": xrp[0],
        "xr_scales": xrp[1],
        "ws_words": wsp[0],
        "ws_scales": wsp[1],
        "offs": striped(idx),
        "offs2": striped8(idx2),
        "offs3": striped(idx3),
        "offs4": striped8(idx4),
        "offs5": striped8(idx5),
        "offs6": striped8(idx6),
        "offs7": striped(idx7),
    }


def reference(xt_words, xt_scales, ua, ha, xo_words, xo_scales, w2_words, w2_scales, sa, sb, wb_words, wb_scales, xr_words, xr_scales, ws_words, ws_scales, offs, offs2, offs3, offs4, offs5, offs6, offs7):
    idx = unstriped(offs)
    idx2 = unstriped8(offs2)
    idx3 = unstriped(offs3)
    idx4 = unstriped8(offs4)
    idx5 = unstriped8(offs5)
    idx6 = unstriped8(offs6)
    idx7 = unstriped(offs7)
    xtu = unpack_weight(xt_words, xt_scales, "e2m1")
    xou = unpack_weight(xo_words, xo_scales, "e4m3")
    w2u = unpack_weight(w2_words, w2_scales, "e2m1")
    wbu = unpack_weight(wb_words, wb_scales, "e2m1")
    xru = unpack_weight(xr_words, xr_scales, "e4m3")
    wsu = unpack_weight(ws_words, ws_scales, "e4m3")
    wc = pick8(f64(ua), idx2, 64) * f64(ha)
    wcq = mxq(wc, 0, "e4m3")
    xtidxg = xtu[:, idx]
    a = wcq.T @ xtidxg
    xoidx3g = xou[:, idx3]
    b = w2u.T @ xoidx3g
    pw = np.zeros((R, C))
    pw[np.arange(R)[:, None], idx4[np.arange(R) % 512 // 64]] = a
    g1 = np.maximum(pick8(pw, idx5, 64) * f64(sa), b)
    hid = pick8(g1, idx6, 64) * f64(sb)
    hidq = mxq(hid, 0, "e4m3")
    xridx7g = xru[:, idx7]
    y = wbu.T @ hidq + wsu.T @ xridx7g
    return y

@@ -1,0 +1,208 @@
+from contextlib import ExitStack
+
+import concourse.mybir as mybir
+
+K, J, R, T, F, Z, M, O, C, N, S, V = 512, 256, 512, 512, 2048, 512, 1024, 128, 512, 256, 512, 1024
+FLOPS = 2 * (K * R * J + Z * R * J + R * N * O + S * N * O)
+
+F32 = mybir.dt.float32
+BF16 = mybir.dt.bfloat16
+I32 = mybir.dt.int32
+U32 = mybir.dt.uint32
+U16 = mybir.dt.uint16
+U8 = mybir.dt.uint8
+FP8X4 = mybir.dt.float8_e4m3fn_x4
+FP4X4 = mybir.dt.float4_e2m1fn_x4
+COPY = mybir.ActivationFunctionType.Copy
+MAX = mybir.AluOpType.max
+
+P = 128
+PACK = 4
+QUADS = 4
+QUAD = P // QUADS
+ROWS = 4
+
+
+def tile_picked_tokens_codes_two_answered_reminder_plain_kernel(
+    tc, xt_words, xt_scales, ua, ha, xo_words, xo_scales, w2_words, w2_scales, sa, sb,
+    wb_words, wb_scales, xr_words, xr_scales, ws_words, ws_scales,
+    offs, offs2, offs3, offs4, offs5, offs6, offs7, out,
+):
+    nc = tc.nc
+    with ExitStack() as ctx:
+        lists = ctx.enter_context(tc.tile_pool(name="lists", bufs=1))
+        sbuf = ctx.enter_context(tc.tile_pool(name="sbuf", bufs=1))
+        psum = ctx.enter_context(tc.psum_pool(name="psum", bufs=1))
+
+        late = ctx.enter_context(tc.tile_pool(name="late", bufs=1))
+
+        def tile(name, shape, dtype, tag=None):
+            return sbuf.tile(shape, dtype, name=name, tag=tag or name, align_bytes=64)
+
+        def load_list(name, src):
+            dst = lists.tile(list(src.shape), U16, name=name)
+            nc.sync.dma_start(dst[:], src)
+            return dst
+
+        def load_rows4(name, src):
+            dst = tile(name, [P, PACK], F32)
+            nc.sync.dma_start(dst[:], src.rearrange("(p t) o -> p (t o)", t=PACK))
+            return dst
+
+        def load_words(name, src, width, dtype):
+            dst = tile(name, [P, width], dtype)
+            nc.sync.dma_start(dst[:].bitcast(I32), src.bitcast(I32))
+            return dst
+
+        def fp8_words(src):
+            return src[0].rearrange("p c t -> p (c t)")
+
+        def zeroed_plane(name, width, tag=None):
+            plane = tile(name, [P, width], U8, tag=tag)
+            nc.vector.memset(plane[:].bitcast(I32), 0)
+            return plane
+
+        def load_plane(plane, src):
+            rows = src[0].rearrange("(q i) c -> i q c", i=ROWS)
+            for i in range(ROWS):
+                nc.sync.dma_start(plane[i:P:QUAD, :].bitcast(I32), rows[i].bitcast(I32))
+
+        def load_staged(name, src, width):
+            staged = tile(name, [ROWS, QUADS, width], U8)
+            nc.sync.dma_start(staged[:].bitcast(I32), src[0].rearrange("(q i) c -> i q c", i=ROWS).bitcast(I32))
+            return staged
+
+        def spread(plane, staged):
+            for q in range(QUADS):
+                nc.vector.tensor_copy(plane[QUAD * q : QUAD * q + ROWS, :].bitcast(I32), staged[:, q, :].bitcast(I32))
+
+        xt_plane = zeroed_plane("xt_plane", T)
+        w2_plane = zeroed_plane("w2_plane", R)
+        xo_plane = zeroed_plane("xo_plane", M, tag="woven0")
+        xr_plane = zeroed_plane("xr_plane", V)
+        ws_plane = zeroed_plane("ws_plane", N)
+        wb_plane = zeroed_plane("wb_plane", N)
+        boards = [tile("board%d" % t, [P, C], F32) for t in range(PACK)]
+        for board in boards:
+            nc.vector.memset(board[:], 0.0)
+
+        ua_rows = ua.rearrange("(p t) f -> p t f", t=PACK)
+        tables = [tile("table%d" % t, [P, F], F32) for t in range(PACK)]
+
+        nc.sync.dma_start(tables[0][:], ua_rows[:, 0, :])
+        l2 = load_list("l2", offs2)
+        ha_sb = load_rows4("ha_sb", ha)
+        nc.sync.dma_start(tables[1][:], ua_rows[:, 1, :])
+        xt_staged = load_staged("xt_staged", xt_scales, T)
+        w2_staged = load_staged("w2_staged", w2_scales, R)
+        l1 = load_list("l1", offs)
+        xt_w = load_words("xt_w", xt_words[0], T, U16)
+        nc.sync.dma_start(tables[2][:], ua_rows[:, 2, :])
+        nc.sync.dma_start(tables[3][:], ua_rows[:, 3, :])
+        l3 = load_list("l3", offs3)
+        load_plane(xo_plane, xo_scales)
+        xo_w = load_words("xo_w", fp8_words(xo_words), M, U32)
+        l4 = load_list("l4", offs4)
+        w2_w = load_words("w2_w", w2_words[0], R, U16)
+        l5 = load_list("l5", offs5)
+        sa_sb = load_rows4("sa_sb", sa)
+        l7 = load_list("l7", offs7)
+        xr_w = load_words("xr_w", fp8_words(xr_words), V, U32)
+        load_plane(xr_plane, xr_scales)
+        ws_w = load_words("ws_w", fp8_words(ws_words), N, U32)
+        load_plane(ws_plane, ws_scales)
+        l6 = load_list("l6", offs6)
+        sb_sb = load_rows4("sb_sb", sb)
+        wb_w = load_words("wb_w", wb_words[0], N, U16)
+        load_plane(wb_plane, wb_scales)
+
+        def gather(dst, window, offsets):
+            nc.vector.tensor_copy(dst[:], window[:].indirect(offsets[:]))
+
+        spread(xt_plane, xt_staged)
+        spread(w2_plane, w2_staged)
+        xt_g = tile("xt_g", [P, J], U16)
+        xt_gs = tile("xt_gs", [P, J], U8)
+        gather(xt_g, xt_w, l1)
+        gather(xt_gs, xt_plane, l1)
+        w2_dealt_s = tile("w2_dealt_s", [P, PACK, P], U8)
+        nc.vector.tensor_copy(w2_dealt_s[:].rearrange("p t m -> p m t"), w2_plane[:].rearrange("p (m t) -> p m t", t=PACK))
+
+        wc = tile("wc", [P, PACK, R], BF16)
+        for t in range(PACK):
+            nc.scalar.activation(wc[:, t, :], tables[t][:].indirect(l2[:]), COPY, scale=ha_sb[:, t : t + 1])
+
+        xo_gs = tile("xo_gs", [P, J], U8)
+        gather(xo_gs, xo_plane, l3)
+
+        wc_view = wc[:].rearrange("p k (m t) -> p m k t", t=PACK)
+        a_ps = [psum.tile([P, J], F32, name="a_ps%d" % t) for t in range(PACK)]
+        a_sb = [tile("a_sb%d" % t, [P, J], F32) for t in range(PACK)]
+        woven = [tile("woven%d" % u, [P, 2, P, PACK], BF16) for u in range(2)]
+        nc.vector.tensor_copy(woven[0][:].rearrange("p t m k -> p m k t"), wc_view[:, :, :, 0:2])
+        nc.scalar.copy(woven[1][:].rearrange("p t m k -> p m k t"), wc_view[:, :, :, 2:4])
+
+        def first_products(u):
+            codes = tile("wc_codes%d" % u, [P, 2, P], U32)
+            scales = tile("wc_scales%d" % u, [P, 2, P], U8)
+            nc.vector.quantize_mx(codes[:].rearrange("p t m -> p (t m)").bitcast(FP8X4), scales[:].rearrange("p t m -> p (t m)"),
+                                  woven[u][:].rearrange("p t m k -> p (t m k)"))
+            for e in range(2):
+                t = 2 * u + e
+                nc.tensor.matmul_mx(a_ps[t][:], lhsT=codes[:, e, :].bitcast(FP8X4), lhsT_scale=scales[:, e, :],
+                                    rhs=xt_g[:].bitcast(FP4X4), rhs_scale=xt_gs[:], start=True, stop=True)
+                nc.scalar.copy(a_sb[t][:], a_ps[t][:])
+
+        first_products(0)
+        xo_g = tile("xo_g", [P, J], U32, tag="woven0")
+        gather(xo_g, xo_w, l3)
+        first_products(1)
+        w2_dealt = tile("w2_dealt", [P, PACK, P], U16, tag="woven1")
+        nc.scalar.copy(w2_dealt[:].rearrange("p t m -> p m t"), w2_w[:].rearrange("p (m t) -> p m t", t=PACK))
+
+        b_ps = [psum.tile([P, 2, J], F32, name="b_ps%d" % h) for h in range(2)]
+        for t in range(PACK):
+            nc.tensor.matmul_mx(b_ps[t // 2][:, t % 2, :], lhsT=w2_dealt[:, t, :].bitcast(FP4X4), lhsT_scale=w2_dealt_s[:, t, :],
+                                rhs=xo_g[:].bitcast(FP8X4), rhs_scale=xo_gs[:], start=True, stop=True)
+
+        fetched = [tile("fetched%d" % t, [P, J], F32) for t in range(PACK - 1)]
+        fetched.append(late.tile([P, J], F32, name="fetched3", offset=0, align_bytes=64))
+
+        def put_and_fetch(t):
+            nc.vector.tensor_copy(boards[t][:].indirect(l4[:]), a_sb[t][:])
+            nc.scalar.activation(fetched[t][:], boards[t][:].indirect(l5[:]), COPY, scale=sa_sb[:, t : t + 1])
+
+        for t in range(PACK):
+            put_and_fetch(t)
+
+        hid = tile("hid", [P, PACK, O], BF16)
+        for t in range(PACK):
+            g1 = tile("g1_%d" % t, [P, J], F32, tag="a_sb3" if t == 1 else None)
+            nc.vector.tensor_tensor(g1[:], fetched[t][:], b_ps[t // 2][:, t % 2, :], MAX)
+            nc.scalar.activation(hid[:, t, :], g1[:].indirect(l6[:]), COPY, scale=sb_sb[:, t : t + 1])
+
+        xr_g = late.tile([P, O], U32, name="xr_g", offset=0, align_bytes=64)
+        xr_gs = late.tile([P, O], U8, name="xr_gs", offset=4 * O, align_bytes=64)
+        gather(xr_g, xr_w, l7)
+        gather(xr_gs, xr_plane, l7)
+        y_ps = [psum.tile([P, O], F32, name="y_ps%d" % h) for h in range(N // P)]
+        for h in range(N // P):
+            cols = slice(h * P, (h + 1) * P)
+            nc.tensor.matmul_mx(y_ps[h][:], lhsT=ws_w[:, cols].bitcast(FP8X4), lhsT_scale=ws_plane[:, cols],
+                                rhs=xr_g[:].bitcast(FP8X4), rhs_scale=xr_gs[:], start=True, stop=False)
+
+        hid_woven = tile("hid_woven", [P, O, PACK], BF16)
+        nc.vector.tensor_copy(hid_woven[:], hid[:].rearrange("p t o -> p o t"))
+        hid_codes = tile("hid_codes", [P, O], U32)
+        hid_scales = tile("hid_scales", [P, O], U8)
+        nc.vector.quantize_mx(hid_codes[:].bitcast(FP8X4), hid_scales[:], hid_woven[:].rearrange("p o t -> p (o t)"))
+        for h in range(N // P):
+            cols = slice(h * P, (h + 1) * P)
+            nc.tensor.matmul_mx(y_ps[h][:], lhsT=wb_w[:, cols].bitcast(FP4X4), lhsT_scale=wb_plane[:, cols],
+                                rhs=hid_codes[:].bitcast(FP8X4), rhs_scale=hid_scales[:], start=False, stop=True)
+        y0 = tile("y0", [P, O], F32)
+        y1 = tile("y1", [P, O], F32)
+        nc.vector.tensor_copy(y0[:], y_ps[0][:])
+        nc.sync.dma_start(out[0:P, :], y0[:])
+        nc.scalar.copy(y1[:], y_ps[1][:])
+        nc.scalar.dma_start(out[P : 2 * P, :], y1[:])

@@ -57,8 +57,8 @@ def tile_picked_tokens_codes_two_answered_reminder_plain_kernel(
         def fp8_words(src):
             return src[0].rearrange("p c t -> p (c t)")
 
-        def zeroed_plane(name, width, tag=None):
-            plane = tile(name, [P, width], U8, tag=tag)
+        def zeroed_plane(name, width):
+            plane = tile(name, [P, width], U8)
             nc.vector.memset(plane[:].bitcast(I32), 0)
             return plane
 
@@ -78,7 +78,7 @@ def tile_picked_tokens_codes_two_answered_reminder_plain_kernel(
 
         xt_plane = zeroed_plane("xt_plane", T)
         w2_plane = zeroed_plane("w2_plane", R)
-        xo_plane = zeroed_plane("xo_plane", M, tag="woven0")
+        xo_plane = zeroed_plane("xo_plane", M)
         xr_plane = zeroed_plane("xr_plane", V)
         ws_plane = zeroed_plane("ws_plane", N)
         wb_plane = zeroed_plane("wb_plane", N)
@@ -93,14 +93,14 @@ def tile_picked_tokens_codes_two_answered_reminder_plain_kernel(
         l2 = load_list("l2", offs2)
         ha_sb = load_rows4("ha_sb", ha)
         nc.sync.dma_start(tables[1][:], ua_rows[:, 1, :])
-        xt_staged = load_staged("xt_staged", xt_scales, T)
-        w2_staged = load_staged("w2_staged", w2_scales, R)
         l1 = load_list("l1", offs)
         xt_w = load_words("xt_w", xt_words[0], T, U16)
+        xt_staged = load_staged("xt_staged", xt_scales, T)
         nc.sync.dma_start(tables[2][:], ua_rows[:, 2, :])
-        nc.sync.dma_start(tables[3][:], ua_rows[:, 3, :])
+        xo_staged = load_staged("xo_staged", xo_scales, M)
         l3 = load_list("l3", offs3)
-        load_plane(xo_plane, xo_scales)
+        w2_staged = load_staged("w2_staged", w2_scales, R)
+        nc.sync.dma_start(tables[3][:], ua_rows[:, 3, :])
         xo_w = load_words("xo_w", fp8_words(xo_words), M, U32)
         l4 = load_list("l4", offs4)
         w2_w = load_words("w2_w", w2_words[0], R, U16)
@@ -120,20 +120,20 @@ def tile_picked_tokens_codes_two_answered_reminder_plain_kernel(
             nc.vector.tensor_copy(dst[:], window[:].indirect(offsets[:]))
 
         spread(xt_plane, xt_staged)
-        spread(w2_plane, w2_staged)
         xt_g = tile("xt_g", [P, J], U16)
         xt_gs = tile("xt_gs", [P, J], U8)
         gather(xt_g, xt_w, l1)
         gather(xt_gs, xt_plane, l1)
+        spread(xo_plane, xo_staged)
+        xo_gs = tile("xo_gs", [P, J], U8)
+        gather(xo_gs, xo_plane, l3)
+        spread(w2_plane, w2_staged)
         w2_dealt_s = tile("w2_dealt_s", [P, PACK, P], U8)
         nc.vector.tensor_copy(w2_dealt_s[:].rearrange("p t m -> p m t"), w2_plane[:].rearrange("p (m t) -> p m t", t=PACK))
 
         wc = tile("wc", [P, PACK, R], BF16)
         for t in range(PACK):
             nc.scalar.activation(wc[:, t, :], tables[t][:].indirect(l2[:]), COPY, scale=ha_sb[:, t : t + 1])
-
-        xo_gs = tile("xo_gs", [P, J], U8)
-        gather(xo_gs, xo_plane, l3)
 
         wc_view = wc[:].rearrange("p k (m t) -> p m k t", t=PACK)
         a_ps = [psum.tile([P, J], F32, name="a_ps%d" % t) for t in range(PACK)]

@@ -39,6 +39,11 @@ def tile_picked_tokens_codes_two_answered_reminder_plain_kernel(
         def tile(name, shape, dtype, tag=None):
             return sbuf.tile(shape, dtype, name=name, tag=tag or name, align_bytes=64)
 
+        mid = ctx.enter_context(tc.tile_pool(name="mid", bufs=1))
+
+        def placed(name, shape, dtype, offset):
+            return mid.tile(shape, dtype, name=name, offset=offset, align_bytes=64)
+
         def load_list(name, src):
             dst = lists.tile(list(src.shape), U16, name=name)
             nc.sync.dma_start(dst[:], src)
@@ -76,9 +81,10 @@ def tile_picked_tokens_codes_two_answered_reminder_plain_kernel(
             for q in range(QUADS):
                 nc.vector.tensor_copy(plane[QUAD * q : QUAD * q + ROWS, :].bitcast(I32), staged[:, q, :].bitcast(I32))
 
+        xo_plane = placed("xo_plane", [P, M], U8, 512)
+        nc.gpsimd.memset(xo_plane[:].bitcast(I32), 0)
         xt_plane = zeroed_plane("xt_plane", T)
         w2_plane = zeroed_plane("w2_plane", R)
-        xo_plane = zeroed_plane("xo_plane", M)
         xr_plane = zeroed_plane("xr_plane", V)
         ws_plane = zeroed_plane("ws_plane", N)
         wb_plane = zeroed_plane("wb_plane", N)
@@ -97,10 +103,10 @@ def tile_picked_tokens_codes_two_answered_reminder_plain_kernel(
         xt_w = load_words("xt_w", xt_words[0], T, U16)
         xt_staged = load_staged("xt_staged", xt_scales, T)
         nc.sync.dma_start(tables[2][:], ua_rows[:, 2, :])
-        xo_staged = load_staged("xo_staged", xo_scales, M)
         l3 = load_list("l3", offs3)
         w2_staged = load_staged("w2_staged", w2_scales, R)
         nc.sync.dma_start(tables[3][:], ua_rows[:, 3, :])
+        load_plane(xo_plane, xo_scales)
         xo_w = load_words("xo_w", fp8_words(xo_words), M, U32)
         l4 = load_list("l4", offs4)
         w2_w = load_words("w2_w", w2_words[0], R, U16)
@@ -124,41 +130,53 @@ def tile_picked_tokens_codes_two_answered_reminder_plain_kernel(
         xt_gs = tile("xt_gs", [P, J], U8)
         gather(xt_g, xt_w, l1)
         gather(xt_gs, xt_plane, l1)
-        spread(xo_plane, xo_staged)
-        xo_gs = tile("xo_gs", [P, J], U8)
-        gather(xo_gs, xo_plane, l3)
         spread(w2_plane, w2_staged)
         w2_dealt_s = tile("w2_dealt_s", [P, PACK, P], U8)
-        nc.vector.tensor_copy(w2_dealt_s[:].rearrange("p t m -> p m t"), w2_plane[:].rearrange("p (m t) -> p m t", t=PACK))
+        nc.vector.tensor_copy(w2_dealt_s[:], w2_plane[:].rearrange("p (m t) -> p t m", t=PACK))
 
         wc = tile("wc", [P, PACK, R], BF16)
         for t in range(PACK):
             nc.scalar.activation(wc[:, t, :], tables[t][:].indirect(l2[:]), COPY, scale=ha_sb[:, t : t + 1])
 
-        wc_view = wc[:].rearrange("p k (m t) -> p m k t", t=PACK)
+        xo_gs = tile("xo_gs", [P, J], U8)
+        gather(xo_gs, xo_plane, l3)
+
+        wc_view = wc[:].rearrange("p k (m t) -> p t m k", t=PACK)
         a_ps = [psum.tile([P, J], F32, name="a_ps%d" % t) for t in range(PACK)]
         a_sb = [tile("a_sb%d" % t, [P, J], F32) for t in range(PACK)]
-        woven = [tile("woven%d" % u, [P, 2, P, PACK], BF16) for u in range(2)]
-        nc.vector.tensor_copy(woven[0][:].rearrange("p t m k -> p m k t"), wc_view[:, :, :, 0:2])
-        nc.scalar.copy(woven[1][:].rearrange("p t m k -> p m k t"), wc_view[:, :, :, 2:4])
 
-        def first_products(u):
-            codes = tile("wc_codes%d" % u, [P, 2, P], U32)
-            scales = tile("wc_scales%d" % u, [P, 2, P], U8)
+        def weave(copy, first, count):
+            if first < 2:
+                woven = placed("woven%d" % first, [P, count, P, PACK], BF16, 1024 * first)
+            else:
+                woven = tile("woven%d" % first, [P, count, P, PACK], BF16)
+            copy(woven[:], wc_view[:, first : first + count])
+            return woven
+
+        def first_products(woven, first, count):
+            if first == 2:
+                codes = placed("wc_codes2", [P, count, P], U32, 1024)
+            else:
+                codes = tile("wc_codes%d" % first, [P, count, P], U32)
+            scales = tile("wc_scales%d" % first, [P, count, P], U8)
             nc.vector.quantize_mx(codes[:].rearrange("p t m -> p (t m)").bitcast(FP8X4), scales[:].rearrange("p t m -> p (t m)"),
-                                  woven[u][:].rearrange("p t m k -> p (t m k)"))
-            for e in range(2):
-                t = 2 * u + e
+                                  woven[:].rearrange("p t m k -> p (t m k)"))
+            for e in range(count):
+                t = first + e
                 nc.tensor.matmul_mx(a_ps[t][:], lhsT=codes[:, e, :].bitcast(FP8X4), lhsT_scale=scales[:, e, :],
                                     rhs=xt_g[:].bitcast(FP4X4), rhs_scale=xt_gs[:], start=True, stop=True)
                 nc.scalar.copy(a_sb[t][:], a_ps[t][:])
 
-        first_products(0)
-        xo_g = tile("xo_g", [P, J], U32, tag="woven0")
+        woven0 = weave(nc.vector.tensor_copy, 0, 1)
+        woven2 = weave(nc.scalar.copy, 2, 2)
+        first_products(woven0, 0, 1)
+        woven1 = weave(nc.vector.tensor_copy, 1, 1)
+        first_products(woven1, 1, 1)
+        xo_g = placed("xo_g", [P, J], U32, 0)
         gather(xo_g, xo_w, l3)
-        first_products(1)
-        w2_dealt = tile("w2_dealt", [P, PACK, P], U16, tag="woven1")
-        nc.scalar.copy(w2_dealt[:].rearrange("p t m -> p m t"), w2_w[:].rearrange("p (m t) -> p m t", t=PACK))
+        first_products(woven2, 2, 2)
+        w2_dealt = tile("w2_dealt", [P, PACK, P], U16, tag="woven2")
+        nc.scalar.copy(w2_dealt[:], w2_w[:].rearrange("p (m t) -> p t m", t=PACK))
 
         b_ps = [psum.tile([P, 2, J], F32, name="b_ps%d" % h) for h in range(2)]
         for t in range(PACK):

@@ -21,6 +21,7 @@ PACK = 4
 QUADS = 4
 QUAD = P // QUADS
 ROWS = 4
+HID_SPLIT = 64
 
 
 def tile_picked_tokens_codes_two_answered_reminder_plain_kernel(
@@ -98,14 +99,14 @@ def tile_picked_tokens_codes_two_answered_reminder_plain_kernel(
         nc.sync.dma_start(tables[0][:], ua_rows[:, 0, :])
         l2 = load_list("l2", offs2)
         ha_sb = load_rows4("ha_sb", ha)
+        xt_staged = load_staged("xt_staged", xt_scales, T)
+        w2_staged = load_staged("w2_staged", w2_scales, R)
         nc.sync.dma_start(tables[1][:], ua_rows[:, 1, :])
         l1 = load_list("l1", offs)
         xt_w = load_words("xt_w", xt_words[0], T, U16)
-        xt_staged = load_staged("xt_staged", xt_scales, T)
         nc.sync.dma_start(tables[2][:], ua_rows[:, 2, :])
-        l3 = load_list("l3", offs3)
-        w2_staged = load_staged("w2_staged", w2_scales, R)
         nc.sync.dma_start(tables[3][:], ua_rows[:, 3, :])
+        l3 = load_list("l3", offs3)
         load_plane(xo_plane, xo_scales)
         xo_w = load_words("xo_w", fp8_words(xo_words), M, U32)
         l4 = load_list("l4", offs4)
@@ -169,8 +170,8 @@ def tile_picked_tokens_codes_two_answered_reminder_plain_kernel(
 
         woven0 = weave(nc.vector.tensor_copy, 0, 1)
         woven2 = weave(nc.scalar.copy, 2, 2)
-        first_products(woven0, 0, 1)
         woven1 = weave(nc.vector.tensor_copy, 1, 1)
+        first_products(woven0, 0, 1)
         first_products(woven1, 1, 1)
         xo_g = placed("xo_g", [P, J], U32, 0)
         gather(xo_g, xo_w, l3)
@@ -190,14 +191,18 @@ def tile_picked_tokens_codes_two_answered_reminder_plain_kernel(
             nc.vector.tensor_copy(boards[t][:].indirect(l4[:]), a_sb[t][:])
             nc.scalar.activation(fetched[t][:], boards[t][:].indirect(l5[:]), COPY, scale=sa_sb[:, t : t + 1])
 
-        for t in range(PACK):
-            put_and_fetch(t)
-
         hid = tile("hid", [P, PACK, O], BF16)
-        for t in range(PACK):
-            g1 = tile("g1_%d" % t, [P, J], F32, tag="a_sb3" if t == 1 else None)
+
+        def answer(t):
+            g1 = tile("g1_%d" % t, [P, J], F32)
             nc.vector.tensor_tensor(g1[:], fetched[t][:], b_ps[t // 2][:, t % 2, :], MAX)
             nc.scalar.activation(hid[:, t, :], g1[:].indirect(l6[:]), COPY, scale=sb_sb[:, t : t + 1])
+
+        for t in range(PACK + 2):
+            if t >= 2:
+                answer(t - 2)
+            if t < PACK:
+                put_and_fetch(t)
 
         xr_g = late.tile([P, O], U32, name="xr_g", offset=0, align_bytes=64)
         xr_gs = late.tile([P, O], U8, name="xr_gs", offset=4 * O, align_bytes=64)
@@ -210,7 +215,9 @@ def tile_picked_tokens_codes_two_answered_reminder_plain_kernel(
                                 rhs=xr_g[:].bitcast(FP8X4), rhs_scale=xr_gs[:], start=True, stop=False)
 
         hid_woven = tile("hid_woven", [P, O, PACK], BF16)
-        nc.vector.tensor_copy(hid_woven[:], hid[:].rearrange("p t o -> p o t"))
+        hid_view = hid[:].rearrange("p t o -> p o t")
+        nc.vector.tensor_copy(hid_woven[:, :HID_SPLIT, :], hid_view[:, :HID_SPLIT, :])
+        nc.scalar.copy(hid_woven[:, HID_SPLIT:, :], hid_view[:, HID_SPLIT:, :])
         hid_codes = tile("hid_codes", [P, O], U32)
         hid_scales = tile("hid_scales", [P, O], U8)
         nc.vector.quantize_mx(hid_codes[:].bitcast(FP8X4), hid_scales[:], hid_woven[:].rearrange("p o t -> p (o t)"))

from contextlib import ExitStack

import concourse.mybir as mybir

K, J, R, T, F, Z, M, O, C, N, S, V = 512, 256, 512, 512, 2048, 512, 1024, 128, 512, 256, 512, 1024
FLOPS = 2 * (K * R * J + Z * R * J + R * N * O + S * N * O)

F32 = mybir.dt.float32
BF16 = mybir.dt.bfloat16
I32 = mybir.dt.int32
U32 = mybir.dt.uint32
U16 = mybir.dt.uint16
U8 = mybir.dt.uint8
FP8X4 = mybir.dt.float8_e4m3fn_x4
FP4X4 = mybir.dt.float4_e2m1fn_x4
COPY = mybir.ActivationFunctionType.Copy
MAX = mybir.AluOpType.max

P = 128
PACK = 4
QUADS = 4
QUAD = P // QUADS
ROWS = 4
HID_SPLIT = 64


def tile_picked_tokens_codes_two_answered_reminder_plain_kernel(
    tc, xt_words, xt_scales, ua, ha, xo_words, xo_scales, w2_words, w2_scales, sa, sb,
    wb_words, wb_scales, xr_words, xr_scales, ws_words, ws_scales,
    offs, offs2, offs3, offs4, offs5, offs6, offs7, out,
):
    nc = tc.nc
    with ExitStack() as ctx:
        lists = ctx.enter_context(tc.tile_pool(name="lists", bufs=1))
        sbuf = ctx.enter_context(tc.tile_pool(name="sbuf", bufs=1))
        psum = ctx.enter_context(tc.psum_pool(name="psum", bufs=1))

        late = ctx.enter_context(tc.tile_pool(name="late", bufs=1))

        def tile(name, shape, dtype, tag=None):
            return sbuf.tile(shape, dtype, name=name, tag=tag or name, align_bytes=64)

        mid = ctx.enter_context(tc.tile_pool(name="mid", bufs=1))

        def placed(name, shape, dtype, offset):
            return mid.tile(shape, dtype, name=name, offset=offset, align_bytes=64)

        def load_list(name, src):
            dst = lists.tile(list(src.shape), U16, name=name)
            nc.sync.dma_start(dst[:], src)
            return dst

        def load_rows4(name, src):
            dst = tile(name, [P, PACK], F32)
            nc.sync.dma_start(dst[:], src.rearrange("(p t) o -> p (t o)", t=PACK))
            return dst

        def load_words(name, src, width, dtype):
            dst = tile(name, [P, width], dtype)
            nc.sync.dma_start(dst[:].bitcast(I32), src.bitcast(I32))
            return dst

        def fp8_words(src):
            return src[0].rearrange("p c t -> p (c t)")

        def zeroed_plane(name, width):
            plane = tile(name, [P, width], U8)
            nc.vector.memset(plane[:].bitcast(I32), 0)
            return plane

        def load_plane(plane, src):
            rows = src[0].rearrange("(q i) c -> i q c", i=ROWS)
            for i in range(ROWS):
                nc.sync.dma_start(plane[i:P:QUAD, :].bitcast(I32), rows[i].bitcast(I32))

        def load_staged(name, src, width):
            staged = tile(name, [ROWS, QUADS, width], U8)
            nc.sync.dma_start(staged[:].bitcast(I32), src[0].rearrange("(q i) c -> i q c", i=ROWS).bitcast(I32))
            return staged

        def spread(plane, staged):
            for q in range(QUADS):
                nc.vector.tensor_copy(plane[QUAD * q : QUAD * q + ROWS, :].bitcast(I32), staged[:, q, :].bitcast(I32))

        xo_plane = placed("xo_plane", [P, M], U8, 512)
        nc.gpsimd.memset(xo_plane[:].bitcast(I32), 0)
        xt_plane = zeroed_plane("xt_plane", T)
        w2_plane = zeroed_plane("w2_plane", R)
        xr_plane = zeroed_plane("xr_plane", V)
        ws_plane = zeroed_plane("ws_plane", N)
        wb_plane = zeroed_plane("wb_plane", N)
        boards = [tile("board%d" % t, [P, C], F32) for t in range(PACK)]
        for board in boards:
            nc.vector.memset(board[:], 0.0)

        ua_rows = ua.rearrange("(p t) f -> p t f", t=PACK)
        tables = [tile("table%d" % t, [P, F], F32) for t in range(PACK)]

        nc.sync.dma_start(tables[0][:], ua_rows[:, 0, :])
        l2 = load_list("l2", offs2)
        ha_sb = load_rows4("ha_sb", ha)
        xt_staged = load_staged("xt_staged", xt_scales, T)
        w2_staged = load_staged("w2_staged", w2_scales, R)
        nc.sync.dma_start(tables[1][:], ua_rows[:, 1, :])
        l1 = load_list("l1", offs)
        xt_w = load_words("xt_w", xt_words[0], T, U16)
        nc.sync.dma_start(tables[2][:], ua_rows[:, 2, :])
        nc.sync.dma_start(tables[3][:], ua_rows[:, 3, :])
        l3 = load_list("l3", offs3)
        load_plane(xo_plane, xo_scales)
        xo_w = load_words("xo_w", fp8_words(xo_words), M, U32)
        l4 = load_list("l4", offs4)
        w2_w = load_words("w2_w", w2_words[0], R, U16)
        l5 = load_list("l5", offs5)
        sa_sb = load_rows4("sa_sb", sa)
        l7 = load_list("l7", offs7)
        xr_w = load_words("xr_w", fp8_words(xr_words), V, U32)
        load_plane(xr_plane, xr_scales)
        ws_w = load_words("ws_w", fp8_words(ws_words), N, U32)
        load_plane(ws_plane, ws_scales)
        l6 = load_list("l6", offs6)
        sb_sb = load_rows4("sb_sb", sb)
        wb_w = load_words("wb_w", wb_words[0], N, U16)
        load_plane(wb_plane, wb_scales)

        def gather(dst, window, offsets):
            nc.vector.tensor_copy(dst[:], window[:].indirect(offsets[:]))

        spread(xt_plane, xt_staged)
        xt_g = tile("xt_g", [P, J], U16)
        xt_gs = tile("xt_gs", [P, J], U8)
        gather(xt_g, xt_w, l1)
        gather(xt_gs, xt_plane, l1)
        spread(w2_plane, w2_staged)
        w2_dealt_s = tile("w2_dealt_s", [P, PACK, P], U8)
        nc.vector.tensor_copy(w2_dealt_s[:], w2_plane[:].rearrange("p (m t) -> p t m", t=PACK))

        wc = tile("wc", [P, PACK, R], BF16)
        for t in range(PACK):
            nc.scalar.activation(wc[:, t, :], tables[t][:].indirect(l2[:]), COPY, scale=ha_sb[:, t : t + 1])

        xo_gs = tile("xo_gs", [P, J], U8)
        gather(xo_gs, xo_plane, l3)

        wc_view = wc[:].rearrange("p k (m t) -> p t m k", t=PACK)
        a_ps = [psum.tile([P, J], F32, name="a_ps%d" % t) for t in range(PACK)]
        a_sb = [tile("a_sb%d" % t, [P, J], F32) for t in range(PACK)]

        def weave(copy, first, count):
            if first < 2:
                woven = placed("woven%d" % first, [P, count, P, PACK], BF16, 1024 * first)
            else:
                woven = tile("woven%d" % first, [P, count, P, PACK], BF16)
            copy(woven[:], wc_view[:, first : first + count])
            return woven

        def first_products(woven, first, count):
            if first == 2:
                codes = placed("wc_codes2", [P, count, P], U32, 1024)
            else:
                codes = tile("wc_codes%d" % first, [P, count, P], U32)
            scales = tile("wc_scales%d" % first, [P, count, P], U8)
            nc.vector.quantize_mx(codes[:].rearrange("p t m -> p (t m)").bitcast(FP8X4), scales[:].rearrange("p t m -> p (t m)"),
                                  woven[:].rearrange("p t m k -> p (t m k)"))
            for e in range(count):
                t = first + e
                nc.tensor.matmul_mx(a_ps[t][:], lhsT=codes[:, e, :].bitcast(FP8X4), lhsT_scale=scales[:, e, :],
                                    rhs=xt_g[:].bitcast(FP4X4), rhs_scale=xt_gs[:], start=True, stop=True)
                nc.scalar.copy(a_sb[t][:], a_ps[t][:])

        woven0 = weave(nc.vector.tensor_copy, 0, 1)
        woven2 = weave(nc.scalar.copy, 2, 2)
        woven1 = weave(nc.vector.tensor_copy, 1, 1)
        first_products(woven0, 0, 1)
        first_products(woven1, 1, 1)
        xo_g = placed("xo_g", [P, J], U32, 0)
        gather(xo_g, xo_w, l3)
        first_products(woven2, 2, 2)
        w2_dealt = tile("w2_dealt", [P, PACK, P], U16, tag="woven2")
        nc.scalar.copy(w2_dealt[:], w2_w[:].rearrange("p (m t) -> p t m", t=PACK))

        b_ps = [psum.tile([P, 2, J], F32, name="b_ps%d" % h) for h in range(2)]
        for t in range(PACK):
            nc.tensor.matmul_mx(b_ps[t // 2][:, t % 2, :], lhsT=w2_dealt[:, t, :].bitcast(FP4X4), lhsT_scale=w2_dealt_s[:, t, :],
                                rhs=xo_g[:].bitcast(FP8X4), rhs_scale=xo_gs[:], start=True, stop=True)

        fetched = [tile("fetched%d" % t, [P, J], F32) for t in range(PACK - 1)]
        fetched.append(late.tile([P, J], F32, name="fetched3", offset=0, align_bytes=64))

        def put_and_fetch(t):
            nc.vector.tensor_copy(boards[t][:].indirect(l4[:]), a_sb[t][:])
            nc.scalar.activation(fetched[t][:], boards[t][:].indirect(l5[:]), COPY, scale=sa_sb[:, t : t + 1])

        hid = tile("hid", [P, PACK, O], BF16)

        def answer(t):
            g1 = tile("g1_%d" % t, [P, J], F32)
            nc.vector.tensor_tensor(g1[:], fetched[t][:], b_ps[t // 2][:, t % 2, :], MAX)
            nc.scalar.activation(hid[:, t, :], g1[:].indirect(l6[:]), COPY, scale=sb_sb[:, t : t + 1])

        for t in range(PACK + 2):
            if t >= 2:
                answer(t - 2)
            if t < PACK:
                put_and_fetch(t)

        xr_g = late.tile([P, O], U32, name="xr_g", offset=0, align_bytes=64)
        xr_gs = late.tile([P, O], U8, name="xr_gs", offset=4 * O, align_bytes=64)
        gather(xr_g, xr_w, l7)
        gather(xr_gs, xr_plane, l7)
        y_ps = [psum.tile([P, O], F32, name="y_ps%d" % h) for h in range(N // P)]
        for h in range(N // P):
            cols = slice(h * P, (h + 1) * P)
            nc.tensor.matmul_mx(y_ps[h][:], lhsT=ws_w[:, cols].bitcast(FP8X4), lhsT_scale=ws_plane[:, cols],
                                rhs=xr_g[:].bitcast(FP8X4), rhs_scale=xr_gs[:], start=True, stop=False)

        hid_woven = tile("hid_woven", [P, O, PACK], BF16)
        hid_view = hid[:].rearrange("p t o -> p o t")
        nc.vector.tensor_copy(hid_woven[:, :HID_SPLIT, :], hid_view[:, :HID_SPLIT, :])
        nc.scalar.copy(hid_woven[:, HID_SPLIT:, :], hid_view[:, HID_SPLIT:, :])
        hid_codes = tile("hid_codes", [P, O], U32)
        hid_scales = tile("hid_scales", [P, O], U8)
        nc.vector.quantize_mx(hid_codes[:].bitcast(FP8X4), hid_scales[:], hid_woven[:].rearrange("p o t -> p (o t)"))
        for h in range(N // P):
            cols = slice(h * P, (h + 1) * P)
            nc.tensor.matmul_mx(y_ps[h][:], lhsT=wb_w[:, cols].bitcast(FP4X4), lhsT_scale=wb_plane[:, cols],
                                rhs=hid_codes[:].bitcast(FP8X4), rhs_scale=hid_scales[:], start=False, stop=True)
        y0 = tile("y0", [P, O], F32)
        y1 = tile("y1", [P, O], F32)
        nc.vector.tensor_copy(y0[:], y_ps[0][:])
        nc.sync.dma_start(out[0:P, :], y0[:])
        nc.scalar.copy(y1[:], y_ps[1][:])
        nc.scalar.dma_start(out[P : 2 * P, :], y1[:])
